import numpy as np
import ml_dtypes


def mxq(x, axis, fmt="e4m3"):
    dtype, down = {"e4m3": (ml_dtypes.float8_e4m3fn, 7), "e5m2": (ml_dtypes.float8_e5m2, 14)}[fmt]
    v = np.moveaxis(np.asarray(x, np.float32).astype(ml_dtypes.bfloat16).astype(np.float64), axis, -1)
    blocks = v.reshape(v.shape[:-1] + (-1, 32))
    amax = np.abs(blocks).max(-1, keepdims=True)
    byte = np.maximum(np.where(amax > 0, np.frexp(amax)[1] - 1 + 127, 0) - down, 1)
    scale = np.exp2(byte - 127.0)
    codes = (blocks / scale).astype(np.float32).astype(dtype).astype(np.float64)
    return np.moveaxis((codes * scale).reshape(v.shape), -1, axis)


WIDE = False


def mx_kscale(k):
    if not WIDE:
        return np.ones(k)
    levels = np.array([10, -10, 5, -5, 0])
    if k % 512:
        return np.exp2(np.random.permutation(np.resize(levels, k // 32))).repeat(32)
    a = np.empty((k // 512, 16))
    for p in range(k // 512):
        a[p, :8] = np.random.permutation(np.resize(levels, 8))
        for g in range(8):
            far = levels[np.abs(levels - a[p, g]) >= 10]
            a[p, g + 8] = far[np.random.randint(len(far))]
    return np.exp2(a.ravel()).repeat(32)


def f64(x):
    return np.asarray(x).astype(np.float64)


def striped(idx):
    return np.tile(idx.reshape(-1, 16).T, (8, 1)).astype(np.uint16)


def unstriped(offs):
    return offs[:16].T.reshape(-1).astype(np.int64)


E2M1 = np.array([0.0, 0.5, 1.0, 1.5, 2.0, 3.0, 4.0, 6.0, -0.0, -0.5, -1.0, -1.5, -2.0, -3.0, -4.0, -6.0])


def pack_weight(w, fmt):
    k, n = w.shape
    w = f64(np.asarray(w, np.float32).astype(ml_dtypes.bfloat16)).reshape(k // 32, 32, n)
    amax = np.abs(w).max(1)
    if fmt == "e4m3":
        byte = np.frexp(amax)[1] - 1 + 127 - 7
    else:
        mant, ex = np.frexp(amax / 6.0)
        byte = np.where(mant > 0.5, ex, ex - 1) + 127
    byte = np.clip(np.where(amax > 0, byte, 1), 1, 254)
    scaled = (w * np.exp2(127.0 - byte)[:, None, :]).reshape(k, n).astype(np.float32)
    by_word = np.ascontiguousarray(scaled.reshape(k // 512, 128, 4, n).transpose(0, 1, 3, 2))
    if fmt == "e4m3":
        words = by_word.astype(ml_dtypes.float8_e4m3fn).view(np.uint8)
    else:
        c = by_word.astype(ml_dtypes.float4_e2m1fn).view(np.uint8) & 0xF
        words = (c[..., 0::2] | (c[..., 1::2] << 4)).reshape(k // 512, 128, 2 * n)
    return np.ascontiguousarray(words), np.ascontiguousarray(byte.astype(np.uint8).reshape(k // 512, 16, n))


def unpack_weight(words, scales, fmt):
    g, _, n = scales.shape
    words = np.ascontiguousarray(words).reshape(g, 128, n, -1)
    if fmt == "e4m3":
        vals = words.view(ml_dtypes.float8_e4m3fn).astype(np.float64)
    else:
        nib = np.empty((g, 128, n, 4), np.uint8)
        nib[..., 0::2] = words & 0xF
        nib[..., 1::2] = words >> 4
        vals = E2M1[nib]
    vals = vals * np.repeat(np.exp2(scales.astype(np.float64) - 127.0), 8, axis=1)[..., None]
    return vals.transpose(0, 1, 3, 2).reshape(g * 512, n)


def gelu(v):
    return 0.5 * v * (1.0 + np.tanh(np.sqrt(2.0 / np.pi) * (v + 0.044715 * v**3)))


K, H, N, T, S, T2, P = 1024, 512, 384, 2048, 1024, 2048, 1024

def setup_inputs():
    n = np.random.standard_normal
    s = mx_kscale(K)[:, None]
    u = mx_kscale(H)[:, None]
    tab_words, tab_scales = pack_weight(n((K, T)) * s, "e4m3")
    w1_words, w1_scales = pack_weight(0.65 * n((K, H)) / np.sqrt(K) / s, "e2m1")
    w4_words, w4_scales = pack_weight(1.5 * n((H, N)) / np.sqrt(H) / u, "e2m1")
    sign = np.random.choice([-1.0, 1.0], H)
    return {
        "tab_words": tab_words, "tab_scales": tab_scales,
        "offs": striped(np.random.permutation(T)[:S]),
        "w1_words": w1_words, "w1_scales": w1_scales,
        "w2": (0.5 * n((K, H)) / np.sqrt(K) / s).astype(np.float32),
        "site": (0.45 * n((H, S))).astype(np.float32),
        "offs2": striped(np.random.permutation(T2)[:S]),
        "wgs": np.exp(0.3 * n((128, S))).astype(np.float32),
        "page0": (0.8 * n((H, T2))).astype(np.float32),
        "offs3": striped(np.random.permutation(T2)[:P]),
        "temp": np.random.uniform(0.4, 1.6, H).astype(np.float32),
        "least": (0.12 * n((H, P))).astype(np.float32),
        "gain": (sign * np.random.uniform(2.5, 5.0, H) * u[:, 0]).astype(np.float32),
        "w3": (1.5 * n((H, N)) / np.sqrt(H) / u).astype(np.float32),
        "w4_words": w4_words, "w4_scales": w4_scales,
        "note": (0.5 * n((N, P))).astype(np.float32),
    }

def reference(tab_words, tab_scales, offs, w1_words, w1_scales, w2, site, offs2, wgs, page0,
              offs3, temp, least, gain, w3, w4_words, w4_scales, note):
    v = unpack_weight(tab_words, tab_scales, "e4m3")[:, unstriped(offs)]
    w1 = unpack_weight(w1_words, w1_scales, "e2m1")
    w4 = unpack_weight(w4_words, w4_scales, "e2m1")
    own = w1.T @ v
    placed = (mxq(f64(w2), 0, "e4m3").T @ v) + f64(site)
    h = np.maximum(own, placed)
    page = f64(page0).copy()
    page[:, unstriped(offs2)] = np.tile(f64(wgs), (H // 128, 1)) * h
    top = page.max(axis=1)
    a = np.exp(f64(temp)[:, None] * (page[:, unstriped(offs3)] - top[:, None]))
    z = mxq(np.maximum(a, f64(least)) * f64(gain)[:, None], 0, "e4m3")
    y1 = mxq(f64(w3), 0, "e4m3").T @ z
    y2 = w4.T @ z
    return np.minimum(y1, y2) + f64(note)

@@ -1,0 +1,276 @@
+from contextlib import ExitStack
+
+import concourse.mybir as mybir
+
+K, H, N, T, S, T2, LOAN = 1024, 512, 384, 2048, 1024, 2048, 1024
+FLOPS = 2 * (2 * K * H * S + 2 * H * N * LOAN)
+
+F32 = mybir.dt.float32
+BF16 = mybir.dt.bfloat16
+I32 = mybir.dt.int32
+U32 = mybir.dt.uint32
+U16 = mybir.dt.uint16
+U8 = mybir.dt.uint8
+FP8X4 = mybir.dt.float8_e4m3fn_x4
+FP4X4 = mybir.dt.float4_e2m1fn_x4
+ALU = mybir.AluOpType
+ACT = mybir.ActivationFunctionType
+AXIS = mybir.AxisListType
+
+P = 128
+PACK = 4
+QUADS = 4
+PASSES = K // (P * PACK)
+BANK = 512
+HALVES = S // BANK
+LIST_COLS = BANK // 16
+N_TILES = N // P
+GPSIMD_SUMS = 4
+
+
+def tile_list_crate_bay_handling_kernel(
+    tc, tab_words, tab_scales, offs, w1_words, w1_scales, w2, site, offs2, wgs, page0,
+    offs3, temp, least, gain, w3, w4_words, w4_scales, note, out,
+):
+    nc = tc.nc
+    with ExitStack() as ctx:
+        keep = ctx.enter_context(tc.tile_pool(name="keep", bufs=1))
+        ring = ctx.enter_context(tc.tile_pool(name="ring", bufs=2))
+        psum = ctx.enter_context(tc.psum_pool(name="psum", bufs=4))
+
+        def tile(name, shape, dtype):
+            return keep.tile(shape, dtype, name=name, align_bytes=64)
+
+        def zeroed(name, shape):
+            plane = tile(name, shape, U8)
+            nc.vector.memset(plane[:].bitcast(I32), 0)
+            return plane
+
+        def load(name, shape, src):
+            dst = tile(name, shape, F32)
+            nc.sync.dma_start(out=dst[:], in_=src)
+            return dst
+
+        def load_list(name, src):
+            dst = keep.tile([P, S // 16], U16, name=name)
+            nc.sync.dma_start(dst[:], src)
+            return dst
+
+        def rows_of(x, t):
+            return x.rearrange("(p t) c -> t p c", t=PACK)[t]
+
+        tab_sc = zeroed("tab_sc", [P, T])
+        w1_sc_raw = zeroed("w1_sc_raw", [P, PASSES * H])
+        pick_sc1 = zeroed("pick_sc1", [P, S])
+        w4_sc = zeroed("w4_sc", [P, N])
+
+        def load_tab_words(a):
+            dst = tile(f"tab_w{a}", [P, T], U32)
+            nc.sync.dma_start(out=dst[:].bitcast(I32), in_=tab_words[a].rearrange("p t i -> p (t i)").bitcast(I32))
+            return dst
+
+        def load_w2(a):
+            return load(f"w2_raw{a}", [P, PACK, H], w2[a * P * PACK:(a + 1) * P * PACK, :].rearrange("(p j) c -> p j c", j=PACK))
+
+        def load_wgs(name, t0, t1):
+            dst = tile(name, [P, (t1 - t0) * S], F32)
+            src = wgs.rearrange("(q t) j -> q (t j)", t=PACK)[:, t0 * S:t1 * S]
+            for quad in range(QUADS):
+                nc.sync.dma_start(out=dst[32 * quad:32 * quad + 32, :], in_=src)
+            return dst
+
+        w2_raw = [load_w2(0)]
+        list1 = load_list("list1", offs)
+        for quad in range(QUADS):
+            nc.sync.dma_start(
+                out=tab_sc[32 * quad:32 * quad + 4 * PASSES, :].bitcast(I32),
+                in_=tab_scales[:, 4 * quad:4 * quad + 4, :].bitcast(I32),
+            )
+        tab_w = [load_tab_words(0)]
+        w1_raw = tile("w1_raw", [P, PASSES, 2 * H], U8)
+        nc.sync.dma_start(out=w1_raw[:].bitcast(I32), in_=w1_words.rearrange("a p c -> p a c").bitcast(I32))
+        w2_raw.append(load_w2(1))
+        tab_w.append(load_tab_words(1))
+        for quad in range(QUADS):
+            nc.sync.dma_start(
+                out=w1_sc_raw[32 * quad:32 * quad + 4, :].rearrange("r (a c) -> r a c", a=PASSES).bitcast(I32),
+                in_=w1_scales[:, 4 * quad:4 * quad + 4, :].rearrange("a r c -> r a c").bitcast(I32),
+            )
+        site_t = [load("site0", [P, S], rows_of(site, 0))]
+        list2 = load_list("list2", offs2)
+        page = [load("page0", [P, T2], rows_of(page0, 0))]
+        wgs_first = load_wgs("wgs_first", 0, 1)
+        list3 = load_list("list3", offs3)
+        temp_c = load("temp_c", [P, PACK], temp.rearrange("(p t) -> p t", t=PACK))
+        gain_c = load("gain_c", [P, PACK], gain.rearrange("(p t) -> p t", t=PACK))
+        site_t.append(load("site1", [P, S], rows_of(site, 1)))
+        wgs_rest = load_wgs("wgs_rest", 1, PACK)
+        page.append(load("page1", [P, T2], rows_of(page0, 1)))
+        least_t = []
+        for t in range(2, PACK):
+            least_t.append(load(f"least{t - 2}", [P, LOAN], rows_of(least, t - 2)))
+            site_t.append(load(f"site{t}", [P, S], rows_of(site, t)))
+            page.append(load(f"page{t}", [P, T2], rows_of(page0, t)))
+        w3_raw = load("w3_raw", [P, PACK, N], w3.rearrange("(p j) n -> p j n", j=PACK))
+        w4_w = tile("w4_w", [P, 2 * N], U8)
+        nc.sync.dma_start(out=w4_w[:].bitcast(I32), in_=w4_words[0].bitcast(I32))
+        for quad in range(QUADS):
+            nc.sync.dma_start(
+                out=w4_sc[32 * quad:32 * quad + 4, :].bitcast(I32),
+                in_=w4_scales[0, 4 * quad:4 * quad + 4, :].bitcast(I32),
+            )
+        for t in range(PACK - 2, PACK):
+            least_t.append(load(f"least{t}", [P, LOAN], rows_of(least, t)))
+        note_t = [load(f"note{i}", [P, LOAN], note[i * P:(i + 1) * P, :]) for i in range(N_TILES)]
+        wgs_t = [wgs_first[:]] + [wgs_rest[:, t * S:(t + 1) * S] for t in range(PACK - 1)]
+
+        pick_sc = tile("pick_sc", [P, S], U8)
+        nc.vector.tensor_copy(pick_sc[:], tab_sc[:].indirect(list1[:]))
+        nc.gpsimd.dma_start(out=pick_sc1[0:100, :].bitcast(I32), in_=pick_sc[4:104, :].bitcast(I32))
+        w1_w = tile("w1_w", [P, PASSES * 2 * H], U8)
+        nc.scalar.copy(
+            out=w1_w[:].bitcast(U16).rearrange("p (a t m) -> p a m t", a=PASSES, t=PACK),
+            in_=w1_raw[:].bitcast(U16).rearrange("p a (m t) -> p a m t", t=PACK),
+        )
+        w1_sc = tile("w1_sc", [P, PASSES * H], U8)
+        nc.vector.tensor_copy(
+            out=w1_sc[:].rearrange("p (a t m) -> p a t m", a=PASSES, t=PACK),
+            in_=w1_sc_raw[:].rearrange("p (a m t) -> p a t m", a=PASSES, t=PACK),
+        )
+
+        pick_w = [[None] * HALVES for a in range(PASSES)]
+        w2_w, w2_sc = [], []
+        for a in range(PASSES):
+            rounded = tile(f"w2_bf{a}", [P, H * PACK], BF16)
+            nc.scalar.activation(
+                out=rounded[:].rearrange("p (t m j) -> p m j t", t=PACK, j=PACK),
+                in_=w2_raw[a][:].rearrange("p j (m t) -> p m j t", t=PACK),
+                func=ACT.Copy,
+            )
+            for c in range(HALVES):
+                pick_w[a][c] = tile(f"pick_w{a}_{c}", [P, BANK], U32)
+                nc.vector.tensor_copy(pick_w[a][c][:], tab_w[a][:].indirect(list1[:, c * LIST_COLS:(c + 1) * LIST_COLS]))
+            w2_w.append(tile(f"w2_w{a}", [P, H], U32))
+            w2_sc.append(tile(f"w2_sc{a}", [P, H], U8))
+            nc.vector.quantize_mx(out=w2_w[a][:].bitcast(FP8X4), scales=w2_sc[a][:], in_=rounded[:])
+
+        neg_temp = tile("neg_temp", [P, PACK], F32)
+        top = tile("top", [P, PACK], F32)
+        shift = tile("shift", [P, PACK], F32)
+        z_bf = [tile(f"z_bf{c}", [P, BANK * PACK], BF16) for c in range(HALVES)]
+        halves = [slice(c * BANK, (c + 1) * BANK) for c in range(HALVES)]
+        h = [[tile(f"h{t}", [P, BANK], F32)[:], least_t[t - 1][:, halves[0]] if t else tile("h0_second", [P, BANK], F32)[:]]
+             for t in range(PACK)]
+        shifted = [h[0]] + [[wgs_t[t - 1][:, halves[1]], h[t - 1][1]] for t in range(1, PACK)]
+        larger = [[h[t + 1][0], shifted[t + 1][1]] for t in range(PACK - 1)]
+        own = {}
+        looked = {}
+
+        def scores(t, c):
+            cols = halves[c]
+            placed = psum.tile([P, BANK], F32, name="bank_a")
+            own[t, c] = psum.tile([P, BANK], F32, name="bank_b")
+            for a in range(PASSES):
+                nc.tensor.matmul_mx(
+                    out=placed[:],
+                    lhsT=w2_w[a][:, t * P:(t + 1) * P].bitcast(FP8X4),
+                    lhsT_scale=w2_sc[a][:, t * P:(t + 1) * P],
+                    rhs=pick_w[a][c][:].bitcast(FP8X4),
+                    rhs_scale=pick_sc[4 * a:P, cols],
+                    start=(a == 0), stop=(a == PASSES - 1),
+                )
+            for a in range(PASSES):
+                nc.tensor.matmul_mx(
+                    out=own[t, c][:],
+                    lhsT=w1_w[:, (a * H + t * P) * 2:(a * H + (t + 1) * P) * 2].bitcast(FP4X4),
+                    lhsT_scale=w1_sc[:, a * H + t * P:a * H + (t + 1) * P],
+                    rhs=pick_w[a][c][:].bitcast(FP8X4),
+                    rhs_scale=(pick_sc, pick_sc1)[a][:, cols],
+                    start=(a == 0), stop=(a == PASSES - 1),
+                )
+            if t == 0:
+                nc.vector.tensor_tensor(shifted[t][c], placed[:], site_t[t][:, cols], ALU.add)
+            else:
+                staged = ring.tile([P, BANK], F32, name="staged", bufs=4)
+                nc.scalar.copy(out=staged[:], in_=placed[:])
+                nc.gpsimd.tensor_tensor(shifted[t][c], staged[:], site_t[t][:, cols], ALU.add)
+
+        def fragility(t, c):
+            nc.vector.tensor_tensor(h[t][c], own[t, c][:], shifted[t][c], ALU.max)
+
+        def put(t, c):
+            nc.vector.tensor_tensor(
+                page[t][:].indirect(list2[:, c * LIST_COLS:(c + 1) * LIST_COLS]),
+                h[t][c], wgs_t[t][:, halves[c]], ALU.mult,
+            )
+
+        def look(t):
+            nc.vector.reduce_max(out=top[:, t:t + 1], in_=page[t][:], axis=AXIS.X)
+            nc.scalar.activation(out=shift[:, t:t + 1], in_=top[:, t:t + 1], func=ACT.Copy, scale=neg_temp[:, t:t + 1])
+            for c in range(HALVES):
+                looked[t, c] = tile(f"looked{c}", [P, BANK], F32)
+                nc.scalar.activation(
+                    out=looked[t, c][:],
+                    in_=page[t][:].indirect(list3[:, c * LIST_COLS:(c + 1) * LIST_COLS]),
+                    func=ACT.Exp, bias=shift[:, t:t + 1], scale=temp_c[:, t:t + 1],
+                )
+
+        def floor_and_gain(t, c):
+            floor = least_t[t][:, halves[c]]
+            dst = z_bf[c][:].rearrange("p (m t) -> p t m", t=PACK)[:, t, :]
+            if t < PACK - 1:
+                nc.vector.tensor_tensor(larger[t][c], looked[t, c][:], floor, ALU.max)
+                nc.scalar.activation(out=dst, in_=larger[t][c], func=ACT.Copy, scale=gain_c[:, t:t + 1])
+            else:
+                nc.vector.tensor_tensor(floor, looked[t, c][:], floor, ALU.max)
+                nc.vector.tensor_scalar(dst, floor, gain_c[:, t:t + 1], None, ALU.mult)
+
+        nc.vector.tensor_scalar(neg_temp[:], temp_c[:], -1.0, None, ALU.mult)
+        w3_w = tile("w3_w", [P, N], U32)
+        w3_sc = tile("w3_sc", [P, N], U8)
+        for t in range(PACK):
+            for c in range(HALVES):
+                scores(t, c)
+            fragility(t, 0)
+            put(t, 0)
+            if t > 0:
+                floor_and_gain(t - 1, 0)
+            fragility(t, 1)
+            if t > 0:
+                floor_and_gain(t - 1, 1)
+            put(t, 1)
+            look(t)
+        w3_bf = tile("w3_bf", [P, N * PACK], BF16)
+        nc.scalar.activation(
+            out=w3_bf[:].rearrange("p (n j) -> p n j", j=PACK),
+            in_=w3_raw[:].rearrange("p j n -> p n j"),
+            func=ACT.Copy,
+        )
+        nc.vector.quantize_mx(out=w3_w[:].bitcast(FP8X4), scales=w3_sc[:], in_=w3_bf[:])
+
+        z_w, z_sc = [], []
+        for c in range(HALVES):
+            floor_and_gain(PACK - 1, c)
+            z_w.append(tile(f"z_w{c}", [P, BANK], U32))
+            z_sc.append(tile(f"z_sc{c}", [P, BANK], U8))
+            nc.vector.quantize_mx(out=z_w[c][:].bitcast(FP8X4), scales=z_sc[c][:], in_=z_bf[c][:])
+
+        for c in range(HALVES):
+            cols = slice(c * BANK, (c + 1) * BANK)
+            for i in range(N_TILES):
+                y1 = psum.tile([P, BANK], F32, name="bank_a")
+                y2 = psum.tile([P, BANK], F32, name="bank_b")
+                nc.tensor.matmul_mx(
+                    out=y1[:], lhsT=w3_w[:, i * P:(i + 1) * P].bitcast(FP8X4), lhsT_scale=w3_sc[:, i * P:(i + 1) * P],
+                    rhs=z_w[c][:].bitcast(FP8X4), rhs_scale=z_sc[c][:], start=True, stop=True,
+                )
+                nc.tensor.matmul_mx(
+                    out=y2[:], lhsT=w4_w[:, i * 2 * P:(i + 1) * 2 * P].bitcast(FP4X4), lhsT_scale=w4_sc[:, i * P:(i + 1) * P],
+                    rhs=z_w[c][:].bitcast(FP8X4), rhs_scale=z_sc[c][:], start=True, stop=True,
+                )
+                lesser = ring.tile([P, BANK], F32, name="lesser", bufs=4)
+                nc.scalar.copy(out=lesser[:], in_=y1[:])
+                nc.vector.tensor_tensor(lesser[:], y2[:], lesser[:], ALU.min)
+                adder = nc.gpsimd if c * N_TILES + i < GPSIMD_SUMS else nc.vector
+                adder.tensor_tensor(note_t[i][:, cols], lesser[:], note_t[i][:, cols], ALU.add)
+                nc.sync.dma_start(out=out[i * P:(i + 1) * P, cols], in_=note_t[i][:, cols])

@@ -25,7 +25,6 @@ BANK = 512
 HALVES = S // BANK
 LIST_COLS = BANK // 16
 N_TILES = N // P
-GPSIMD_SUMS = 4
 
 
 def tile_list_crate_bay_handling_kernel(
@@ -72,9 +71,9 @@ def tile_list_crate_bay_handling_kernel(
         def load_w2(a):
             return load(f"w2_raw{a}", [P, PACK, H], w2[a * P * PACK:(a + 1) * P * PACK, :].rearrange("(p j) c -> p j c", j=PACK))
 
-        def load_wgs(name, t0, t1):
-            dst = tile(name, [P, (t1 - t0) * S], F32)
-            src = wgs.rearrange("(q t) j -> q (t j)", t=PACK)[:, t0 * S:t1 * S]
+        def load_wgs(name, c0, c1):
+            dst = tile(name, [P, c1 - c0], F32)
+            src = wgs.rearrange("(q t) j -> q (t j)", t=PACK)[:, c0:c1]
             for quad in range(QUADS):
                 nc.sync.dma_start(out=dst[32 * quad:32 * quad + 32, :], in_=src)
             return dst
@@ -96,20 +95,22 @@ def tile_list_crate_bay_handling_kernel(
                 out=w1_sc_raw[32 * quad:32 * quad + 4, :].rearrange("r (a c) -> r a c", a=PASSES).bitcast(I32),
                 in_=w1_scales[:, 4 * quad:4 * quad + 4, :].rearrange("a r c -> r a c").bitcast(I32),
             )
-        site_t = [load("site0", [P, S], rows_of(site, 0))]
+        site_first = [load("site0_0", [P, BANK], rows_of(site, 0)[:, 0:BANK])]
         list2 = load_list("list2", offs2)
+        wgs_first = [load_wgs("wgs0_0", 0, BANK)]
         page = [load("page0", [P, T2], rows_of(page0, 0))]
-        wgs_first = load_wgs("wgs_first", 0, 1)
+        site_first.append(load("site0_1", [P, BANK], rows_of(site, 0)[:, BANK:S]))
+        wgs_first.append(load_wgs("wgs0_1", BANK, S))
         list3 = load_list("list3", offs3)
         temp_c = load("temp_c", [P, PACK], temp.rearrange("(p t) -> p t", t=PACK))
         gain_c = load("gain_c", [P, PACK], gain.rearrange("(p t) -> p t", t=PACK))
-        site_t.append(load("site1", [P, S], rows_of(site, 1)))
-        wgs_rest = load_wgs("wgs_rest", 1, PACK)
+        site_t = [None, load("site1", [P, S], rows_of(site, 1))]
+        wgs_rest = load_wgs("wgs_rest", S, PACK * S)
         page.append(load("page1", [P, T2], rows_of(page0, 1)))
         least_t = []
         for t in range(2, PACK):
-            least_t.append(load(f"least{t - 2}", [P, LOAN], rows_of(least, t - 2)))
             site_t.append(load(f"site{t}", [P, S], rows_of(site, t)))
+            least_t.append(load(f"least{t - 2}", [P, LOAN], rows_of(least, t - 2)))
             page.append(load(f"page{t}", [P, T2], rows_of(page0, t)))
         w3_raw = load("w3_raw", [P, PACK, N], w3.rearrange("(p j) n -> p j n", j=PACK))
         w4_w = tile("w4_w", [P, 2 * N], U8)
@@ -122,7 +123,6 @@ def tile_list_crate_bay_handling_kernel(
         for t in range(PACK - 2, PACK):
             least_t.append(load(f"least{t}", [P, LOAN], rows_of(least, t)))
         note_t = [load(f"note{i}", [P, LOAN], note[i * P:(i + 1) * P, :]) for i in range(N_TILES)]
-        wgs_t = [wgs_first[:]] + [wgs_rest[:, t * S:(t + 1) * S] for t in range(PACK - 1)]
 
         pick_sc = tile("pick_sc", [P, S], U8)
         nc.vector.tensor_copy(pick_sc[:], tab_sc[:].indirect(list1[:]))
@@ -159,17 +159,12 @@ def tile_list_crate_bay_handling_kernel(
         shift = tile("shift", [P, PACK], F32)
         z_bf = [tile(f"z_bf{c}", [P, BANK * PACK], BF16) for c in range(HALVES)]
         halves = [slice(c * BANK, (c + 1) * BANK) for c in range(HALVES)]
-        h = [[tile(f"h{t}", [P, BANK], F32)[:], least_t[t - 1][:, halves[0]] if t else tile("h0_second", [P, BANK], F32)[:]]
-             for t in range(PACK)]
-        shifted = [h[0]] + [[wgs_t[t - 1][:, halves[1]], h[t - 1][1]] for t in range(1, PACK)]
-        larger = [[h[t + 1][0], shifted[t + 1][1]] for t in range(PACK - 1)]
-        own = {}
         looked = {}
 
-        def scores(t, c):
+        def scores(t, c, h):
             cols = halves[c]
             placed = psum.tile([P, BANK], F32, name="bank_a")
-            own[t, c] = psum.tile([P, BANK], F32, name="bank_b")
+            own = psum.tile([P, BANK], F32, name="bank_b")
             for a in range(PASSES):
                 nc.tensor.matmul_mx(
                     out=placed[:],
@@ -181,34 +176,21 @@ def tile_list_crate_bay_handling_kernel(
                 )
             for a in range(PASSES):
                 nc.tensor.matmul_mx(
-                    out=own[t, c][:],
+                    out=own[:],
                     lhsT=w1_w[:, (a * H + t * P) * 2:(a * H + (t + 1) * P) * 2].bitcast(FP4X4),
                     lhsT_scale=w1_sc[:, a * H + t * P:a * H + (t + 1) * P],
                     rhs=pick_w[a][c][:].bitcast(FP8X4),
                     rhs_scale=(pick_sc, pick_sc1)[a][:, cols],
                     start=(a == 0), stop=(a == PASSES - 1),
                 )
-            if t == 0:
-                nc.vector.tensor_tensor(shifted[t][c], placed[:], site_t[t][:, cols], ALU.add)
-            else:
-                staged = ring.tile([P, BANK], F32, name="staged", bufs=4)
-                nc.scalar.copy(out=staged[:], in_=placed[:])
-                nc.gpsimd.tensor_tensor(shifted[t][c], staged[:], site_t[t][:, cols], ALU.add)
-
-        def fragility(t, c):
-            nc.vector.tensor_tensor(h[t][c], own[t, c][:], shifted[t][c], ALU.max)
-
-        def put(t, c):
-            nc.vector.tensor_tensor(
-                page[t][:].indirect(list2[:, c * LIST_COLS:(c + 1) * LIST_COLS]),
-                h[t][c], wgs_t[t][:, halves[c]], ALU.mult,
-            )
+            nc.vector.tensor_tensor(h[:, cols], placed[:], site_t[t][:, cols] if t else site_first[c][:], ALU.add)
+            nc.vector.tensor_tensor(h[:, cols], own[:], h[:, cols], ALU.max)
 
         def look(t):
             nc.vector.reduce_max(out=top[:, t:t + 1], in_=page[t][:], axis=AXIS.X)
             nc.scalar.activation(out=shift[:, t:t + 1], in_=top[:, t:t + 1], func=ACT.Copy, scale=neg_temp[:, t:t + 1])
             for c in range(HALVES):
-                looked[t, c] = tile(f"looked{c}", [P, BANK], F32)
+                looked[t, c] = ring.tile([P, BANK], F32, name=f"looked{c}")
                 nc.scalar.activation(
                     out=looked[t, c][:],
                     in_=page[t][:].indirect(list3[:, c * LIST_COLS:(c + 1) * LIST_COLS]),
@@ -218,28 +200,28 @@ def tile_list_crate_bay_handling_kernel(
         def floor_and_gain(t, c):
             floor = least_t[t][:, halves[c]]
             dst = z_bf[c][:].rearrange("p (m t) -> p t m", t=PACK)[:, t, :]
-            if t < PACK - 1:
-                nc.vector.tensor_tensor(larger[t][c], looked[t, c][:], floor, ALU.max)
-                nc.scalar.activation(out=dst, in_=larger[t][c], func=ACT.Copy, scale=gain_c[:, t:t + 1])
+            nc.vector.tensor_tensor(floor, looked[t, c][:], floor, ALU.max)
+            if t < 2:
+                nc.scalar.activation(out=dst, in_=floor, func=ACT.Copy, scale=gain_c[:, t:t + 1])
             else:
-                nc.vector.tensor_tensor(floor, looked[t, c][:], floor, ALU.max)
                 nc.vector.tensor_scalar(dst, floor, gain_c[:, t:t + 1], None, ALU.mult)
 
         nc.vector.tensor_scalar(neg_temp[:], temp_c[:], -1.0, None, ALU.mult)
         w3_w = tile("w3_w", [P, N], U32)
         w3_sc = tile("w3_sc", [P, N], U8)
         for t in range(PACK):
+            h = ring.tile([P, S], F32, name="h")
             for c in range(HALVES):
-                scores(t, c)
-            fragility(t, 0)
-            put(t, 0)
+                scores(t, c, h)
+                if t == 0:
+                    nc.vector.tensor_tensor(
+                        page[t][:].indirect(list2[:, c * LIST_COLS:(c + 1) * LIST_COLS]), h[:, halves[c]], wgs_first[c][:], ALU.mult)
             if t > 0:
-                floor_and_gain(t - 1, 0)
-            fragility(t, 1)
-            if t > 0:
-                floor_and_gain(t - 1, 1)
-            put(t, 1)
+                nc.vector.tensor_tensor(page[t][:].indirect(list2[:]), h[:], wgs_rest[:, (t - 1) * S:t * S], ALU.mult)
             look(t)
+            if t > 0:
+                for c in range(HALVES):
+                    floor_and_gain(t - 1, c)
         w3_bf = tile("w3_bf", [P, N * PACK], BF16)
         nc.scalar.activation(
             out=w3_bf[:].rearrange("p (n j) -> p n j", j=PACK),
@@ -271,6 +253,5 @@ def tile_list_crate_bay_handling_kernel(
                 lesser = ring.tile([P, BANK], F32, name="lesser", bufs=4)
                 nc.scalar.copy(out=lesser[:], in_=y1[:])
                 nc.vector.tensor_tensor(lesser[:], y2[:], lesser[:], ALU.min)
-                adder = nc.gpsimd if c * N_TILES + i < GPSIMD_SUMS else nc.vector
-                adder.tensor_tensor(note_t[i][:, cols], lesser[:], note_t[i][:, cols], ALU.add)
+                nc.vector.tensor_tensor(note_t[i][:, cols], lesser[:], note_t[i][:, cols], ALU.add)
                 nc.sync.dma_start(out=out[i * P:(i + 1) * P, cols], in_=note_t[i][:, cols])

@@ -15,7 +15,6 @@ FP8X4 = mybir.dt.float8_e4m3fn_x4
 FP4X4 = mybir.dt.float4_e2m1fn_x4
 ALU = mybir.AluOpType
 ACT = mybir.ActivationFunctionType
-AXIS = mybir.AxisListType
 
 P = 128
 PACK = 4
@@ -89,12 +88,12 @@ def tile_list_crate_bay_handling_kernel(
         w1_raw = tile("w1_raw", [P, PASSES, 2 * H], U8)
         nc.sync.dma_start(out=w1_raw[:].bitcast(I32), in_=w1_words.rearrange("a p c -> p a c").bitcast(I32))
         w2_raw.append(load_w2(1))
-        tab_w.append(load_tab_words(1))
         for quad in range(QUADS):
             nc.sync.dma_start(
                 out=w1_sc_raw[32 * quad:32 * quad + 4, :].rearrange("r (a c) -> r a c", a=PASSES).bitcast(I32),
                 in_=w1_scales[:, 4 * quad:4 * quad + 4, :].rearrange("a r c -> r a c").bitcast(I32),
             )
+        tab_w.append(load_tab_words(1))
         site_first = [load("site0_0", [P, BANK], rows_of(site, 0)[:, 0:BANK])]
         list2 = load_list("list2", offs2)
         wgs_first = [load_wgs("wgs0_0", 0, BANK)]
@@ -155,7 +154,7 @@ def tile_list_crate_bay_handling_kernel(
             nc.vector.quantize_mx(out=w2_w[a][:].bitcast(FP8X4), scales=w2_sc[a][:], in_=rounded[:])
 
         neg_temp = tile("neg_temp", [P, PACK], F32)
-        top = tile("top", [P, PACK], F32)
+        scaled = tile("scaled", [P, T2], F32)
         shift = tile("shift", [P, PACK], F32)
         z_bf = [tile(f"z_bf{c}", [P, BANK * PACK], BF16) for c in range(HALVES)]
         halves = [slice(c * BANK, (c + 1) * BANK) for c in range(HALVES)]
@@ -183,12 +182,16 @@ def tile_list_crate_bay_handling_kernel(
                     rhs_scale=(pick_sc, pick_sc1)[a][:, cols],
                     start=(a == 0), stop=(a == PASSES - 1),
                 )
-            nc.vector.tensor_tensor(h[:, cols], placed[:], site_t[t][:, cols] if t else site_first[c][:], ALU.add)
+            if t == 0:
+                nc.vector.tensor_tensor(h[:, cols], placed[:], site_first[c][:], ALU.add)
+            else:
+                staged = ring.tile([P, BANK], F32, name="staged", bufs=4)
+                nc.scalar.copy(out=staged[:], in_=placed[:])
+                nc.gpsimd.tensor_tensor(h[:, cols], staged[:], site_t[t][:, cols], ALU.add)
             nc.vector.tensor_tensor(h[:, cols], own[:], h[:, cols], ALU.max)
 
         def look(t):
-            nc.vector.reduce_max(out=top[:, t:t + 1], in_=page[t][:], axis=AXIS.X)
-            nc.scalar.activation(out=shift[:, t:t + 1], in_=top[:, t:t + 1], func=ACT.Copy, scale=neg_temp[:, t:t + 1])
+            nc.vector.tensor_scalar(scaled[:], page[t][:], neg_temp[:, t:t + 1], None, ALU.mult, ALU.min, accum_out=shift[:, t:t + 1])
             for c in range(HALVES):
                 looked[t, c] = ring.tile([P, BANK], F32, name=f"looked{c}")
                 nc.scalar.activation(
@@ -209,16 +212,19 @@ def tile_list_crate_bay_handling_kernel(
         nc.vector.tensor_scalar(neg_temp[:], temp_c[:], -1.0, None, ALU.mult)
         w3_w = tile("w3_w", [P, N], U32)
         w3_sc = tile("w3_sc", [P, N], U8)
+        h = tile("h", [P, S], F32)
+        for c in range(HALVES):
+            scores(0, c, h)
+            nc.vector.tensor_tensor(
+                page[0][:].indirect(list2[:, c * LIST_COLS:(c + 1) * LIST_COLS]), h[:, halves[c]], wgs_first[c][:], ALU.mult)
         for t in range(PACK):
-            h = ring.tile([P, S], F32, name="h")
-            for c in range(HALVES):
-                scores(t, c, h)
-                if t == 0:
-                    nc.vector.tensor_tensor(
-                        page[t][:].indirect(list2[:, c * LIST_COLS:(c + 1) * LIST_COLS]), h[:, halves[c]], wgs_first[c][:], ALU.mult)
             if t > 0:
                 nc.vector.tensor_tensor(page[t][:].indirect(list2[:]), h[:], wgs_rest[:, (t - 1) * S:t * S], ALU.mult)
             look(t)
+            if t + 1 < PACK:
+                h = tile("h", [P, S], F32)
+                for c in range(HALVES):
+                    scores(t + 1, c, h)
             if t > 0:
                 for c in range(HALVES):
                     floor_and_gain(t - 1, c)

from contextlib import ExitStack

import concourse.mybir as mybir

K, H, N, T, S, T2, LOAN = 1024, 512, 384, 2048, 1024, 2048, 1024
FLOPS = 2 * (2 * K * H * S + 2 * H * N * LOAN)

F32 = mybir.dt.float32
BF16 = mybir.dt.bfloat16
I32 = mybir.dt.int32
U32 = mybir.dt.uint32
U16 = mybir.dt.uint16
U8 = mybir.dt.uint8
FP8X4 = mybir.dt.float8_e4m3fn_x4
FP4X4 = mybir.dt.float4_e2m1fn_x4
ALU = mybir.AluOpType
ACT = mybir.ActivationFunctionType

P = 128
PACK = 4
QUADS = 4
PASSES = K // (P * PACK)
BANK = 512
HALVES = S // BANK
LIST_COLS = BANK // 16
N_TILES = N // P


def tile_list_crate_bay_handling_kernel(
    tc, tab_words, tab_scales, offs, w1_words, w1_scales, w2, site, offs2, wgs, page0,
    offs3, temp, least, gain, w3, w4_words, w4_scales, note, out,
):
    nc = tc.nc
    with ExitStack() as ctx:
        keep = ctx.enter_context(tc.tile_pool(name="keep", bufs=1))
        ring = ctx.enter_context(tc.tile_pool(name="ring", bufs=2))
        psum = ctx.enter_context(tc.psum_pool(name="psum", bufs=4))

        def tile(name, shape, dtype):
            return keep.tile(shape, dtype, name=name, align_bytes=64)

        def zeroed(name, shape):
            plane = tile(name, shape, U8)
            nc.vector.memset(plane[:].bitcast(I32), 0)
            return plane

        def load(name, shape, src):
            dst = tile(name, shape, F32)
            nc.sync.dma_start(out=dst[:], in_=src)
            return dst

        def load_list(name, src):
            dst = keep.tile([P, S // 16], U16, name=name)
            nc.sync.dma_start(dst[:], src)
            return dst

        def rows_of(x, t):
            return x.rearrange("(p t) c -> t p c", t=PACK)[t]

        tab_sc = zeroed("tab_sc", [P, T])
        w1_sc_raw = zeroed("w1_sc_raw", [P, PASSES * H])
        pick_sc1 = zeroed("pick_sc1", [P, S])
        w4_sc = zeroed("w4_sc", [P, N])

        def load_tab_words(a):
            dst = tile(f"tab_w{a}", [P, T], U32)
            nc.sync.dma_start(out=dst[:].bitcast(I32), in_=tab_words[a].rearrange("p t i -> p (t i)").bitcast(I32))
            return dst

        def load_w2(a):
            return load(f"w2_raw{a}", [P, PACK, H], w2[a * P * PACK:(a + 1) * P * PACK, :].rearrange("(p j) c -> p j c", j=PACK))

        def load_wgs(name, c0, c1):
            dst = tile(name, [P, c1 - c0], F32)
            src = wgs.rearrange("(q t) j -> q (t j)", t=PACK)[:, c0:c1]
            for quad in range(QUADS):
                nc.sync.dma_start(out=dst[32 * quad:32 * quad + 32, :], in_=src)
            return dst

        w2_raw = [load_w2(0)]
        list1 = load_list("list1", offs)
        for quad in range(QUADS):
            nc.sync.dma_start(
                out=tab_sc[32 * quad:32 * quad + 4 * PASSES, :].bitcast(I32),
                in_=tab_scales[:, 4 * quad:4 * quad + 4, :].bitcast(I32),
            )
        tab_w = [load_tab_words(0)]
        w1_raw = tile("w1_raw", [P, PASSES, 2 * H], U8)
        nc.sync.dma_start(out=w1_raw[:].bitcast(I32), in_=w1_words.rearrange("a p c -> p a c").bitcast(I32))
        w2_raw.append(load_w2(1))
        for quad in range(QUADS):
            nc.sync.dma_start(
                out=w1_sc_raw[32 * quad:32 * quad + 4, :].rearrange("r (a c) -> r a c", a=PASSES).bitcast(I32),
                in_=w1_scales[:, 4 * quad:4 * quad + 4, :].rearrange("a r c -> r a c").bitcast(I32),
            )
        tab_w.append(load_tab_words(1))
        site_first = [load("site0_0", [P, BANK], rows_of(site, 0)[:, 0:BANK])]
        list2 = load_list("list2", offs2)
        wgs_first = [load_wgs("wgs0_0", 0, BANK)]
        page = [load("page0", [P, T2], rows_of(page0, 0))]
        site_first.append(load("site0_1", [P, BANK], rows_of(site, 0)[:, BANK:S]))
        wgs_first.append(load_wgs("wgs0_1", BANK, S))
        list3 = load_list("list3", offs3)
        temp_c = load("temp_c", [P, PACK], temp.rearrange("(p t) -> p t", t=PACK))
        gain_c = load("gain_c", [P, PACK], gain.rearrange("(p t) -> p t", t=PACK))
        site_t = [None, load("site1", [P, S], rows_of(site, 1))]
        wgs_rest = load_wgs("wgs_rest", S, PACK * S)
        page.append(load("page1", [P, T2], rows_of(page0, 1)))
        least_t = []
        for t in range(2, PACK):
            site_t.append(load(f"site{t}", [P, S], rows_of(site, t)))
            least_t.append(load(f"least{t - 2}", [P, LOAN], rows_of(least, t - 2)))
            page.append(load(f"page{t}", [P, T2], rows_of(page0, t)))
        w3_raw = load("w3_raw", [P, PACK, N], w3.rearrange("(p j) n -> p j n", j=PACK))
        w4_w = tile("w4_w", [P, 2 * N], U8)
        nc.sync.dma_start(out=w4_w[:].bitcast(I32), in_=w4_words[0].bitcast(I32))
        for quad in range(QUADS):
            nc.sync.dma_start(
                out=w4_sc[32 * quad:32 * quad + 4, :].bitcast(I32),
                in_=w4_scales[0, 4 * quad:4 * quad + 4, :].bitcast(I32),
            )
        for t in range(PACK - 2, PACK):
            least_t.append(load(f"least{t}", [P, LOAN], rows_of(least, t)))
        note_t = [load(f"note{i}", [P, LOAN], note[i * P:(i + 1) * P, :]) for i in range(N_TILES)]

        pick_sc = tile("pick_sc", [P, S], U8)
        nc.vector.tensor_copy(pick_sc[:], tab_sc[:].indirect(list1[:]))
        nc.gpsimd.dma_start(out=pick_sc1[0:100, :].bitcast(I32), in_=pick_sc[4:104, :].bitcast(I32))
        w1_w = tile("w1_w", [P, PASSES * 2 * H], U8)
        nc.scalar.copy(
            out=w1_w[:].bitcast(U16).rearrange("p (a t m) -> p a m t", a=PASSES, t=PACK),
            in_=w1_raw[:].bitcast(U16).rearrange("p a (m t) -> p a m t", t=PACK),
        )
        w1_sc = tile("w1_sc", [P, PASSES * H], U8)
        nc.vector.tensor_copy(
            out=w1_sc[:].rearrange("p (a t m) -> p a t m", a=PASSES, t=PACK),
            in_=w1_sc_raw[:].rearrange("p (a m t) -> p a t m", a=PASSES, t=PACK),
        )

        pick_w = [[None] * HALVES for a in range(PASSES)]
        w2_w, w2_sc = [], []
        for a in range(PASSES):
            rounded = tile(f"w2_bf{a}", [P, H * PACK], BF16)
            nc.scalar.activation(
                out=rounded[:].rearrange("p (t m j) -> p m j t", t=PACK, j=PACK),
                in_=w2_raw[a][:].rearrange("p j (m t) -> p m j t", t=PACK),
                func=ACT.Copy,
            )
            for c in range(HALVES):
                pick_w[a][c] = tile(f"pick_w{a}_{c}", [P, BANK], U32)
                nc.vector.tensor_copy(pick_w[a][c][:], tab_w[a][:].indirect(list1[:, c * LIST_COLS:(c + 1) * LIST_COLS]))
            w2_w.append(tile(f"w2_w{a}", [P, H], U32))
            w2_sc.append(tile(f"w2_sc{a}", [P, H], U8))
            nc.vector.quantize_mx(out=w2_w[a][:].bitcast(FP8X4), scales=w2_sc[a][:], in_=rounded[:])

        neg_temp = tile("neg_temp", [P, PACK], F32)
        scaled = tile("scaled", [P, T2], F32)
        shift = tile("shift", [P, PACK], F32)
        z_bf = [tile(f"z_bf{c}", [P, BANK * PACK], BF16) for c in range(HALVES)]
        halves = [slice(c * BANK, (c + 1) * BANK) for c in range(HALVES)]
        looked = {}

        def scores(t, c, h):
            cols = halves[c]
            placed = psum.tile([P, BANK], F32, name="bank_a")
            own = psum.tile([P, BANK], F32, name="bank_b")
            for a in range(PASSES):
                nc.tensor.matmul_mx(
                    out=placed[:],
                    lhsT=w2_w[a][:, t * P:(t + 1) * P].bitcast(FP8X4),
                    lhsT_scale=w2_sc[a][:, t * P:(t + 1) * P],
                    rhs=pick_w[a][c][:].bitcast(FP8X4),
                    rhs_scale=pick_sc[4 * a:P, cols],
                    start=(a == 0), stop=(a == PASSES - 1),
                )
            for a in range(PASSES):
                nc.tensor.matmul_mx(
                    out=own[:],
                    lhsT=w1_w[:, (a * H + t * P) * 2:(a * H + (t + 1) * P) * 2].bitcast(FP4X4),
                    lhsT_scale=w1_sc[:, a * H + t * P:a * H + (t + 1) * P],
                    rhs=pick_w[a][c][:].bitcast(FP8X4),
                    rhs_scale=(pick_sc, pick_sc1)[a][:, cols],
                    start=(a == 0), stop=(a == PASSES - 1),
                )
            if t == 0:
                nc.vector.tensor_tensor(h[:, cols], placed[:], site_first[c][:], ALU.add)
            else:
                staged = ring.tile([P, BANK], F32, name="staged", bufs=4)
                nc.scalar.copy(out=staged[:], in_=placed[:])
                nc.gpsimd.tensor_tensor(h[:, cols], staged[:], site_t[t][:, cols], ALU.add)
            nc.vector.tensor_tensor(h[:, cols], own[:], h[:, cols], ALU.max)

        def look(t):
            nc.vector.tensor_scalar(scaled[:], page[t][:], neg_temp[:, t:t + 1], None, ALU.mult, ALU.min, accum_out=shift[:, t:t + 1])
            for c in range(HALVES):
                looked[t, c] = ring.tile([P, BANK], F32, name=f"looked{c}")
                nc.scalar.activation(
                    out=looked[t, c][:],
                    in_=page[t][:].indirect(list3[:, c * LIST_COLS:(c + 1) * LIST_COLS]),
                    func=ACT.Exp, bias=shift[:, t:t + 1], scale=temp_c[:, t:t + 1],
                )

        def floor_and_gain(t, c):
            floor = least_t[t][:, halves[c]]
            dst = z_bf[c][:].rearrange("p (m t) -> p t m", t=PACK)[:, t, :]
            nc.vector.tensor_tensor(floor, looked[t, c][:], floor, ALU.max)
            if t < 2:
                nc.scalar.activation(out=dst, in_=floor, func=ACT.Copy, scale=gain_c[:, t:t + 1])
            else:
                nc.vector.tensor_scalar(dst, floor, gain_c[:, t:t + 1], None, ALU.mult)

        nc.vector.tensor_scalar(neg_temp[:], temp_c[:], -1.0, None, ALU.mult)
        w3_w = tile("w3_w", [P, N], U32)
        w3_sc = tile("w3_sc", [P, N], U8)
        h = tile("h", [P, S], F32)
        for c in range(HALVES):
            scores(0, c, h)
            nc.vector.tensor_tensor(
                page[0][:].indirect(list2[:, c * LIST_COLS:(c + 1) * LIST_COLS]), h[:, halves[c]], wgs_first[c][:], ALU.mult)
        for t in range(PACK):
            if t > 0:
                nc.vector.tensor_tensor(page[t][:].indirect(list2[:]), h[:], wgs_rest[:, (t - 1) * S:t * S], ALU.mult)
            look(t)
            if t + 1 < PACK:
                h = tile("h", [P, S], F32)
                for c in range(HALVES):
                    scores(t + 1, c, h)
            if t > 0:
                for c in range(HALVES):
                    floor_and_gain(t - 1, c)
        w3_bf = tile("w3_bf", [P, N * PACK], BF16)
        nc.scalar.activation(
            out=w3_bf[:].rearrange("p (n j) -> p n j", j=PACK),
            in_=w3_raw[:].rearrange("p j n -> p n j"),
            func=ACT.Copy,
        )
        nc.vector.quantize_mx(out=w3_w[:].bitcast(FP8X4), scales=w3_sc[:], in_=w3_bf[:])

        z_w, z_sc = [], []
        for c in range(HALVES):
            floor_and_gain(PACK - 1, c)
            z_w.append(tile(f"z_w{c}", [P, BANK], U32))
            z_sc.append(tile(f"z_sc{c}", [P, BANK], U8))
            nc.vector.quantize_mx(out=z_w[c][:].bitcast(FP8X4), scales=z_sc[c][:], in_=z_bf[c][:])

        for c in range(HALVES):
            cols = slice(c * BANK, (c + 1) * BANK)
            for i in range(N_TILES):
                y1 = psum.tile([P, BANK], F32, name="bank_a")
                y2 = psum.tile([P, BANK], F32, name="bank_b")
                nc.tensor.matmul_mx(
                    out=y1[:], lhsT=w3_w[:, i * P:(i + 1) * P].bitcast(FP8X4), lhsT_scale=w3_sc[:, i * P:(i + 1) * P],
                    rhs=z_w[c][:].bitcast(FP8X4), rhs_scale=z_sc[c][:], start=True, stop=True,
                )
                nc.tensor.matmul_mx(
                    out=y2[:], lhsT=w4_w[:, i * 2 * P:(i + 1) * 2 * P].bitcast(FP4X4), lhsT_scale=w4_sc[:, i * P:(i + 1) * P],
                    rhs=z_w[c][:].bitcast(FP8X4), rhs_scale=z_sc[c][:], start=True, stop=True,
                )
                lesser = ring.tile([P, BANK], F32, name="lesser", bufs=4)
                nc.scalar.copy(out=lesser[:], in_=y1[:])
                nc.vector.tensor_tensor(lesser[:], y2[:], lesser[:], ALU.min)
                nc.vector.tensor_tensor(note_t[i][:, cols], lesser[:], note_t[i][:, cols], ALU.add)
                nc.sync.dma_start(out=out[i * P:(i + 1) * P, cols], in_=note_t[i][:, cols])
